import numpy as np
import ml_dtypes


def mxq(x, axis, fmt="e4m3"):
    dtype, down = {"e4m3": (ml_dtypes.float8_e4m3fn, 7), "e5m2": (ml_dtypes.float8_e5m2, 14)}[fmt]
    v = np.moveaxis(np.asarray(x, np.float32).astype(ml_dtypes.bfloat16).astype(np.float64), axis, -1)
    blocks = v.reshape(v.shape[:-1] + (-1, 32))
    amax = np.abs(blocks).max(-1, keepdims=True)
    byte = np.maximum(np.where(amax > 0, np.frexp(amax)[1] - 1 + 127, 0) - down, 1)
    scale = np.exp2(byte - 127.0)
    codes = (blocks / scale).astype(np.float32).astype(dtype).astype(np.float64)
    return np.moveaxis((codes * scale).reshape(v.shape), -1, axis)


WIDE = False


def mx_kscale(k):
    if not WIDE:
        return np.ones(k)
    levels = np.array([30, -30])
    if k % 512:
        return np.exp2(np.random.permutation(np.resize(levels, k // 32))).repeat(32)
    a = np.empty((k // 512, 16))
    for p in range(k // 512):
        a[p, :8] = np.random.permutation(np.resize(levels, 8))
        for g in range(8):
            far = levels[np.abs(levels - a[p, g]) >= 10]
            a[p, g + 8] = far[np.random.randint(len(far))]
    return np.exp2(a.ravel()).repeat(32)


def f64(x):
    return np.asarray(x).astype(np.float64)


def striped(idx):
    return np.tile(np.asarray(idx).reshape(-1, 16).T, (8, 1)).astype(np.uint16)


def unstriped(offs):
    return offs[:16].T.reshape(-1).astype(np.int64)


E2M1 = np.array([0.0, 0.5, 1.0, 1.5, 2.0, 3.0, 4.0, 6.0, -0.0, -0.5, -1.0, -1.5, -2.0, -3.0, -4.0, -6.0])


def pack_weight(w, fmt):
    k, n = w.shape
    w = f64(np.asarray(w, np.float32).astype(ml_dtypes.bfloat16)).reshape(k // 32, 32, n)
    amax = np.abs(w).max(1)
    if fmt == "e4m3":
        byte = np.frexp(amax)[1] - 1 + 127 - 7
    else:
        mant, ex = np.frexp(amax / 6.0)
        byte = np.where(mant > 0.5, ex, ex - 1) + 127
    byte = np.clip(np.where(amax > 0, byte, 1), 1, 254)
    scaled = (w * np.exp2(127.0 - byte)[:, None, :]).reshape(k, n).astype(np.float32)
    by_word = np.ascontiguousarray(scaled.reshape(k // 512, 128, 4, n).transpose(0, 1, 3, 2))
    if fmt == "e4m3":
        words = by_word.astype(ml_dtypes.float8_e4m3fn).view(np.uint8)
    else:
        c = by_word.astype(ml_dtypes.float4_e2m1fn).view(np.uint8) & 0xF
        words = (c[..., 0::2] | (c[..., 1::2] << 4)).reshape(k // 512, 128, 2 * n)
    return np.ascontiguousarray(words), np.ascontiguousarray(byte.astype(np.uint8).reshape(k // 512, 16, n))


def unpack_weight(words, scales, fmt):
    g, _, n = scales.shape
    words = np.ascontiguousarray(words).reshape(g, 128, n, -1)
    if fmt == "e4m3":
        vals = words.view(ml_dtypes.float8_e4m3fn).astype(np.float64)
    else:
        nib = np.empty((g, 128, n, 4), np.uint8)
        nib[..., 0::2] = words & 0xF
        nib[..., 1::2] = words >> 4
        vals = E2M1[nib]
    vals = vals * np.repeat(np.exp2(scales.astype(np.float64) - 127.0), 8, axis=1)[..., None]
    return vals.transpose(0, 1, 3, 2).reshape(g * 512, n)


def bf(x):
    return np.asarray(x, np.float32).astype(ml_dtypes.bfloat16)


def planes(Y):
    r, m = Y.shape
    b = f64(bf(Y)).reshape(r // 32, 32, m)
    amax = np.abs(b).max(1)
    byte = np.clip(np.where(amax > 0, np.frexp(amax)[1] - 1 + 127 - 7, 1), 1, 254)
    codes = (b * np.exp2(127.0 - byte)[:, None, :]).reshape(r, m).astype(np.float32).astype(ml_dtypes.float8_e4m3fn).view(np.uint8)
    words = codes.reshape(r // 512, 128, 4, m).transpose(0, 1, 3, 2)
    return np.ascontiguousarray(words), np.ascontiguousarray(byte.astype(np.uint8).reshape(r // 512, 16, m))


K, T, J, R, G, N, E = 1024, 1024, 256, 512, 32, 512, 64


def setup_inputs():
    n = np.random.standard_normal
    idx = np.random.permutation(T)[:J]
    idx2 = np.random.permutation(J)[:E]
    idx3 = np.random.permutation(J)[:E]
    fk = mx_kscale(K)
    fr = mx_kscale(R)
    wp = pack_weight(n((K, R)) * 1 / np.sqrt(K) * fk[:, None] * fr, "e4m3")
    wbp = pack_weight(n((R, N)) * 1 / np.sqrt(R) / fr[:, None], "e2m1")
    return {
        "xf": (n((K, T))).astype(np.float32),
        "fk": (np.random.uniform(0.5, 2.0, (K, 1)) / fk[:, None]).astype(np.float32),
        "w_words": wp[0],
        "w_scales": wp[1],
        "wb_words": wbp[0],
        "wb_scales": wbp[1],
        "gm": (np.random.uniform(0.5, 2.0, (N, 1))).astype(np.float32),
        "offs": striped(idx),
        "offs2": striped(idx2),
        "offs3": striped(idx3),
    }


def reference(xf, fk, w_words, w_scales, wb_words, wb_scales, gm, offs, offs2, offs3):
    idx = unstriped(offs)
    idx2 = unstriped(offs2)
    idx3 = unstriped(offs3)
    wu = unpack_weight(w_words, w_scales, "e4m3")
    wbu = unpack_weight(wb_words, wb_scales, "e2m1")
    xg = f64(xf)[:, idx]
    x1 = np.pad(xg, ((0, 0), (1, 0)))[:, :J]
    u = (xg - 0.6 * x1) * f64(fk)
    uq = mxq(u, 0, "e4m3")
    a = wu.T @ uq
    m1 = a.reshape(R, G, J // G).mean(axis=2)
    m2 = np.repeat(m1, J // G, axis=1)
    hid = a - m2
    hidq = mxq(hid, 0, "e5m2")
    p = wbu.T @ hidq
    y = (p[:, idx2] - p[:, idx3]) * f64(gm)
    words, scales = planes(y)
    return y, words, scales

@@ -1,0 +1,199 @@
+from contextlib import ExitStack
+
+import concourse.mybir as mybir
+
+K, T, J, R, N, E = 1024, 1024, 256, 512, 512, 64
+FLOPS = 2 * K * R * J + 2 * R * N * J
+
+F32 = mybir.dt.float32
+BF16 = mybir.dt.bfloat16
+I32 = mybir.dt.int32
+U32 = mybir.dt.uint32
+U16 = mybir.dt.uint16
+U8 = mybir.dt.uint8
+E4M3 = mybir.dt.float8_e4m3fn_x4
+E5M2 = mybir.dt.float8_e5m2_x4
+E2M1 = mybir.dt.float4_e2m1fn_x4
+MULT = mybir.AluOpType.mult
+ADD = mybir.AluOpType.add
+SUB = mybir.AluOpType.subtract
+COPY = mybir.ActivationFunctionType.Copy
+
+P = 128
+PACK = 4
+PASSES = K // (P * PACK)
+HALF = J // 2
+BUNDLE = 8
+PAD = 8
+
+
+def tile_list_steps_levelled_pickgap_pl_kernel(
+    tc, xf, fk, w_words, w_scales, wb_words, wb_scales, gm, offs, offs2, offs3, out_0, out_1, out_2
+):
+    nc = tc.nc
+    with ExitStack() as ctx:
+        sb = ctx.enter_context(tc.tile_pool(name="sb", bufs=1))
+        ps = ctx.enter_context(tc.psum_pool(name="ps", bufs=1))
+
+        def tile(name, shape, dtype):
+            return sb.tile(shape, dtype, name=name, align_bytes=64)
+
+        list1 = tile("list1", [P, J // 16], U16)
+        nc.sync.dma_start(list1[:], offs)
+
+        scales_raw = tile("scales_raw", [P, R], U8)
+        nc.gpsimd.memset(scales_raw[:].bitcast(I32), 0)
+        fk_sb = tile("fk_sb", [P, PASSES, PACK], F32)
+        nc.gpsimd.dma_start(fk_sb[:], fk.rearrange("(a p i) o -> p a (i o)", a=PASSES, i=PACK))
+        for q in range(4):
+            nc.gpsimd.dma_start(
+                scales_raw[32 * q + 4 : 32 * q + 12, :].bitcast(I32),
+                w_scales[:, 4 * q : 4 * q + 4, :].bitcast(I32),
+            )
+        for q in range(4):
+            nc.gpsimd.dma_start(
+                scales_raw[32 * q : 32 * q + 4, :].bitcast(I32),
+                wb_scales[0, 4 * q : 4 * q + 4, :].bitcast(I32),
+            )
+
+        w_raw = tile("w_raw", [P, PASSES, R], I32)
+        nc.sync.dma_start(w_raw[:], w_words.rearrange("a p n t -> p a (n t)").bitcast(I32))
+        wb_raw = tile("wb_raw", [P, 2 * N], U8)
+        nc.sync.dma_start(wb_raw[:].bitcast(I32), wb_words[0].bitcast(I32))
+
+        planes = xf.rearrange("(a p i) t -> a i p t", a=PASSES, i=PACK)
+        x_sb = {}
+        for a in range(PASSES):
+            for i in range(PACK):
+                x_sb[a, i] = tile("x%d%d" % (a, i), [P, T], F32)
+                nc.sync.dma_start(x_sb[a, i][:], planes[a, i])
+
+        list2 = tile("list2", [P, E // 16], U16)
+        nc.sync.dma_start(list2[:], offs2)
+        list3 = tile("list3", [P, E // 16], U16)
+        nc.sync.dma_start(list3[:], offs3)
+        gm_sb = tile("gm_sb", [P, PACK], F32)
+        nc.sync.dma_start(gm_sb[:], gm.rearrange("(p t) o -> p (t o)", t=PACK))
+
+        w_dealt = tile("w_dealt", [P, PASSES, R], I32)
+        for a in range(PASSES):
+            nc.vector.tensor_copy(
+                w_dealt[:, a, :].rearrange("p (t m) -> p m t", t=PACK),
+                w_raw[:, a, :].rearrange("p (m t) -> p m t", t=PACK),
+            )
+        wb_dealt = tile("wb_dealt", [P, 2 * N], U8)
+        nc.vector.tensor_copy(
+            wb_dealt[:].rearrange("p (t m b) -> p m t b", t=PACK, b=2),
+            wb_raw[:].rearrange("p (m t b) -> p m t b", t=PACK, b=2),
+        )
+        scales_dealt = tile("scales_dealt", [P, R], U8)
+        nc.vector.tensor_copy(
+            scales_dealt[:].rearrange("p (t m) -> p m t", t=PACK),
+            scales_raw[:].rearrange("p (m t) -> p m t", t=PACK),
+        )
+
+        acc_a = [ps.tile([P, PACK, HALF], F32, name="acc_a%d" % h) for h in range(2)]
+        for a in range(PASSES):
+            u_bf = [tile("u%d%d" % (a, h), [P, HALF, PACK], BF16) for h in range(2)]
+            for i in range(PACK):
+                last = a == PASSES - 1 and i == PACK - 1
+                xg = tile("xg%d%d" % (a, i), [P, PAD + J], F32)
+                nc.vector.memset(xg[:, PAD - 1 : PAD], 0.0)
+                window = x_sb[a, i][:]
+                step = tile("step%d%d" % (a, i), [P, J], F32)
+                if last:
+                    nc.scalar.activation(xg[:, PAD : PAD + HALF], window.indirect(list1[:, 0:8]), COPY)
+                    nc.vector.tensor_copy(xg[:, PAD + HALF :], window.indirect(list1[:, 8:16]))
+                    pieces = [(0, HALF), (HALF, J)]
+                else:
+                    nc.scalar.activation(xg[:, PAD:], window.indirect(list1[:]), COPY)
+                    pieces = [(0, J)]
+                for lo, hi in pieces:
+                    nc.vector.scalar_tensor_tensor(
+                        step[:, lo:hi], xg[:, PAD - 1 + lo : PAD - 1 + hi], -0.6, xg[:, PAD + lo : PAD + hi], MULT, ADD
+                    )
+                for h in range(2):
+                    nc.vector.tensor_scalar(
+                        u_bf[h][:, :, i], step[:, h * HALF : (h + 1) * HALF], fk_sb[:, a, i : i + 1], None, MULT
+                    )
+            for h in range(2):
+                u_codes = tile("uc%d%d" % (a, h), [P, HALF], U32)
+                u_scales = tile("us%d%d" % (a, h), [P, HALF], U8)
+                nc.vector.quantize_mx(u_codes[:].bitcast(E4M3), u_scales[:], u_bf[h][:].rearrange("p j t -> p (j t)"))
+                for t in range(PACK):
+                    cols = slice(t * P, (t + 1) * P)
+                    nc.tensor.matmul_mx(
+                        acc_a[h][:, t, :],
+                        lhsT=w_dealt[:, a, cols].bitcast(E4M3),
+                        lhsT_scale=scales_dealt[4 + 4 * a :, cols],
+                        rhs=u_codes[:].bitcast(E4M3),
+                        rhs_scale=u_scales[:],
+                        start=(a == 0 and t == 0),
+                        stop=(a == PASSES - 1 and t == PACK - 1),
+                    )
+
+        groups = HALF // BUNDLE
+        means = []
+        for h in range(2):
+            sums = tile("sums%d" % h, [P, groups, PACK], F32)
+            nc.vector.tensor_reduce(
+                sums[:], acc_a[h][:].rearrange("p t (g s) -> p g t s", s=BUNDLE), mybir.AxisListType.X, ADD
+            )
+            mean = tile("mean%d" % h, [P, groups, PACK], F32)
+            nc.scalar.activation(mean[:], sums[:], COPY, scale=1.0 / BUNDLE)
+            means.append(mean)
+
+        p_sb = [tile("p%d" % t, [P, J], F32) for t in range(PACK)]
+        acc_p0 = ps.tile([P, PACK, HALF], F32, name="acc_p0")
+        acc_p1 = [ps.tile([P, HALF], F32, name="acc_p1%d" % t) for t in range(PACK)]
+        for h in range(2):
+            hid_bf = tile("hid%d" % h, [P, HALF, PACK], BF16)
+            nc.vector.tensor_tensor(
+                hid_bf[:].rearrange("p (g s) t -> p g s t", s=BUNDLE),
+                acc_a[h][:].rearrange("p t (g s) -> p g s t", s=BUNDLE),
+                means[h][:].unsqueeze(2).to_broadcast([P, groups, BUNDLE, PACK]),
+                SUB,
+            )
+            h_codes = tile("hc%d" % h, [P, HALF], U32)
+            h_scales = tile("hs%d" % h, [P, HALF], U8)
+            nc.vector.quantize_mx(h_codes[:].bitcast(E5M2), h_scales[:], hid_bf[:].rearrange("p j t -> p (j t)"))
+            for t in range(PACK):
+                target = acc_p0[:, t, :] if h == 0 else acc_p1[t][:]
+                nc.tensor.matmul_mx(
+                    target,
+                    lhsT=wb_dealt[:, 2 * t * P : 2 * (t + 1) * P].bitcast(E2M1),
+                    lhsT_scale=scales_dealt[:, t * P : (t + 1) * P],
+                    rhs=h_codes[:].bitcast(E5M2),
+                    rhs_scale=h_scales[:],
+                    start=True,
+                    stop=True,
+                )
+            for t in range(PACK):
+                if h == 0:
+                    nc.scalar.copy(p_sb[t][:, :HALF], acc_p0[:, t, :])
+                elif t % 2 == 0:
+                    nc.vector.tensor_copy(p_sb[t][:, HALF:], acc_p1[t][:])
+                else:
+                    nc.scalar.copy(p_sb[t][:, HALF:], acc_p1[t][:])
+
+        first = tile("first", [P, PACK, E], F32)
+        second = tile("second", [P, PACK, E], F32)
+        for t in range(PACK):
+            nc.vector.tensor_copy(first[:, t, :], p_sb[t][:].indirect(list2[:]))
+            nc.scalar.activation(second[:, t, :], p_sb[t][:].indirect(list3[:]), COPY)
+        gap = tile("gap", [P, PACK, E], F32)
+        nc.vector.tensor_tensor(gap[:], first[:], second[:], SUB)
+        y = tile("y", [P, PACK, E], F32)
+        nc.vector.tensor_tensor(y[:], gap[:], gm_sb[:].unsqueeze(2).to_broadcast([P, PACK, E]), MULT)
+        nc.sync.dma_start(out_0.rearrange("(p t) e -> p t e", t=PACK), y[:])
+        y_bf = tile("y_bf", [P, E, PACK], BF16)
+        nc.vector.tensor_copy(y_bf[:], y[:].rearrange("p t e -> p e t"))
+        y_codes = tile("y_codes", [P, E], U32)
+        y_scales = tile("y_scales", [P, E], U8)
+        nc.vector.quantize_mx(y_codes[:].bitcast(E4M3), y_scales[:], y_bf[:].rearrange("p e t -> p (e t)"))
+        nc.scalar.dma_start(out_1[0].rearrange("p c r -> p (c r)").bitcast(I32), y_codes[:].bitcast(I32))
+        for q in range(4):
+            queue = nc.sync if q % 2 == 0 else nc.scalar
+            queue.dma_start(
+                out_2[0, 4 * q : 4 * q + 4, :].bitcast(I32), y_scales[32 * q : 32 * q + 4, :].bitcast(I32)
+            )

@@ -40,40 +40,51 @@ def tile_list_steps_levelled_pickgap_pl_kernel(
 
         list1 = tile("list1", [P, J // 16], U16)
         nc.sync.dma_start(list1[:], offs)
-
         scales_raw = tile("scales_raw", [P, R], U8)
         nc.gpsimd.memset(scales_raw[:].bitcast(I32), 0)
         fk_sb = tile("fk_sb", [P, PASSES, PACK], F32)
         nc.gpsimd.dma_start(fk_sb[:], fk.rearrange("(a p i) o -> p a (i o)", a=PASSES, i=PACK))
-        for q in range(4):
-            nc.gpsimd.dma_start(
-                scales_raw[32 * q + 4 : 32 * q + 12, :].bitcast(I32),
-                w_scales[:, 4 * q : 4 * q + 4, :].bitcast(I32),
-            )
-        for q in range(4):
-            nc.gpsimd.dma_start(
-                scales_raw[32 * q : 32 * q + 4, :].bitcast(I32),
-                wb_scales[0, 4 * q : 4 * q + 4, :].bitcast(I32),
-            )
-
-        w_raw = tile("w_raw", [P, PASSES, R], I32)
-        nc.sync.dma_start(w_raw[:], w_words.rearrange("a p n t -> p a (n t)").bitcast(I32))
-        wb_raw = tile("wb_raw", [P, 2 * N], U8)
-        nc.sync.dma_start(wb_raw[:].bitcast(I32), wb_words[0].bitcast(I32))
+        gm_sb = tile("gm_sb", [P, PACK], F32)
+        nc.gpsimd.dma_start(gm_sb[:], gm.rearrange("(p t) o -> p (t o)", t=PACK))
 
         planes = xf.rearrange("(a p i) t -> a i p t", a=PASSES, i=PACK)
-        x_sb = {}
-        for a in range(PASSES):
-            for i in range(PACK):
-                x_sb[a, i] = tile("x%d%d" % (a, i), [P, T], F32)
-                nc.sync.dma_start(x_sb[a, i][:], planes[a, i])
+        x_sb = {(a, i): tile("x%d%d" % (a, i), [P, T], F32) for a in range(PASSES) for i in range(PACK)}
+        w_raw = tile("w_raw", [P, PASSES, R], I32)
+        wb_raw = tile("wb_raw", [P, 2 * N], U8)
 
+        def load_plane(a, i):
+            nc.sync.dma_start(x_sb[a, i][:], planes[a, i])
+
+        def load_w_scales(q):
+            nc.sync.dma_start(
+                scales_raw[32 * q + 4 : 32 * q + 12, :].bitcast(I32), w_scales[:, 4 * q : 4 * q + 4, :].bitcast(I32)
+            )
+
+        def load_wb_scales(q):
+            nc.sync.dma_start(
+                scales_raw[32 * q : 32 * q + 4, :].bitcast(I32), wb_scales[0, 4 * q : 4 * q + 4, :].bitcast(I32)
+            )
+
+        load_plane(0, 0)
+        load_w_scales(0)
+        nc.sync.dma_start(w_raw[:], w_words.rearrange("a p n t -> p a (n t)").bitcast(I32))
+        load_w_scales(1)
+        nc.sync.dma_start(wb_raw[:].bitcast(I32), wb_words[0].bitcast(I32))
+        load_w_scales(2)
+        load_plane(0, 1)
+        load_w_scales(3)
+        load_plane(0, 2)
+        load_wb_scales(0)
+        load_wb_scales(1)
+        load_plane(0, 3)
+        load_wb_scales(2)
+        load_wb_scales(3)
+        for i in range(PACK):
+            load_plane(1, i)
         list2 = tile("list2", [P, E // 16], U16)
         nc.sync.dma_start(list2[:], offs2)
         list3 = tile("list3", [P, E // 16], U16)
         nc.sync.dma_start(list3[:], offs3)
-        gm_sb = tile("gm_sb", [P, PACK], F32)
-        nc.sync.dma_start(gm_sb[:], gm.rearrange("(p t) o -> p (t o)", t=PACK))
 
         w_dealt = tile("w_dealt", [P, PASSES, R], I32)
         for a in range(PASSES):
@@ -83,54 +94,59 @@ def tile_list_steps_levelled_pickgap_pl_kernel(
             )
         wb_dealt = tile("wb_dealt", [P, 2 * N], U8)
         nc.vector.tensor_copy(
-            wb_dealt[:].rearrange("p (t m b) -> p m t b", t=PACK, b=2),
-            wb_raw[:].rearrange("p (m t b) -> p m t b", t=PACK, b=2),
+            wb_dealt[:].bitcast(U16).rearrange("p (t m) -> p m t", t=PACK),
+            wb_raw[:].bitcast(U16).rearrange("p (m t) -> p m t", t=PACK),
         )
         scales_dealt = tile("scales_dealt", [P, R], U8)
         nc.vector.tensor_copy(
-            scales_dealt[:].rearrange("p (t m) -> p m t", t=PACK),
-            scales_raw[:].rearrange("p (m t) -> p m t", t=PACK),
+            scales_dealt[:].rearrange("p (t m) -> p t m", t=PACK),
+            scales_raw[:].rearrange("p (m t) -> p t m", t=PACK),
         )
 
         acc_a = [ps.tile([P, PACK, HALF], F32, name="acc_a%d" % h) for h in range(2)]
+        xg = tile("xg", [P, PASSES * PACK, PAD + J], F32)
+        nc.vector.memset(xg[:, :, PAD - 1 : PAD], 0.0)
+
+        def take_step(dst, row, lo, hi):
+            nc.vector.scalar_tensor_tensor(
+                dst, xg[:, row, PAD - 1 + lo : PAD - 1 + hi], -0.6, xg[:, row, PAD + lo : PAD + hi], MULT, ADD
+            )
+
+        def first_product(a, h, codes, scales):
+            for t in range(PACK):
+                cols = slice(t * P, (t + 1) * P)
+                nc.tensor.matmul_mx(
+                    acc_a[h][:, t, :],
+                    lhsT=w_dealt[:, a, cols].bitcast(E4M3),
+                    lhsT_scale=scales_dealt[4 + 4 * a :, cols],
+                    rhs=codes.bitcast(E4M3),
+                    rhs_scale=scales,
+                    start=(a == 0 and t == 0),
+                    stop=(a == PASSES - 1 and t == PACK - 1),
+                )
+
+        steps = tile("steps", [P, PASSES * PACK, J], F32)
         for a in range(PASSES):
             u_bf = [tile("u%d%d" % (a, h), [P, HALF, PACK], BF16) for h in range(2)]
             for i in range(PACK):
-                last = a == PASSES - 1 and i == PACK - 1
-                xg = tile("xg%d%d" % (a, i), [P, PAD + J], F32)
-                nc.vector.memset(xg[:, PAD - 1 : PAD], 0.0)
+                row = a * PACK + i
                 window = x_sb[a, i][:]
-                step = tile("step%d%d" % (a, i), [P, J], F32)
-                if last:
-                    nc.scalar.activation(xg[:, PAD : PAD + HALF], window.indirect(list1[:, 0:8]), COPY)
-                    nc.vector.tensor_copy(xg[:, PAD + HALF :], window.indirect(list1[:, 8:16]))
-                    pieces = [(0, HALF), (HALF, J)]
+                if row == PASSES * PACK - 1:
+                    nc.scalar.activation(xg[:, row, PAD : PAD + HALF], window.indirect(list1[:, 0:8]), COPY)
+                    nc.vector.tensor_copy(xg[:, row, PAD + HALF :], window.indirect(list1[:, 8:16]))
                 else:
-                    nc.scalar.activation(xg[:, PAD:], window.indirect(list1[:]), COPY)
-                    pieces = [(0, J)]
-                for lo, hi in pieces:
-                    nc.vector.scalar_tensor_tensor(
-                        step[:, lo:hi], xg[:, PAD - 1 + lo : PAD - 1 + hi], -0.6, xg[:, PAD + lo : PAD + hi], MULT, ADD
-                    )
+                    nc.scalar.activation(xg[:, row, PAD:], window.indirect(list1[:]), COPY)
+                for h in range(2):
+                    take_step(steps[:, row, h * HALF : (h + 1) * HALF], row, h * HALF, (h + 1) * HALF)
                 for h in range(2):
                     nc.vector.tensor_scalar(
-                        u_bf[h][:, :, i], step[:, h * HALF : (h + 1) * HALF], fk_sb[:, a, i : i + 1], None, MULT
+                        u_bf[h][:, :, i], steps[:, row, h * HALF : (h + 1) * HALF], fk_sb[:, a, i : i + 1], None, MULT
                     )
             for h in range(2):
                 u_codes = tile("uc%d%d" % (a, h), [P, HALF], U32)
                 u_scales = tile("us%d%d" % (a, h), [P, HALF], U8)
                 nc.vector.quantize_mx(u_codes[:].bitcast(E4M3), u_scales[:], u_bf[h][:].rearrange("p j t -> p (j t)"))
-                for t in range(PACK):
-                    cols = slice(t * P, (t + 1) * P)
-                    nc.tensor.matmul_mx(
-                        acc_a[h][:, t, :],
-                        lhsT=w_dealt[:, a, cols].bitcast(E4M3),
-                        lhsT_scale=scales_dealt[4 + 4 * a :, cols],
-                        rhs=u_codes[:].bitcast(E4M3),
-                        rhs_scale=u_scales[:],
-                        start=(a == 0 and t == 0),
-                        stop=(a == PASSES - 1 and t == PACK - 1),
-                    )
+                first_product(a, h, u_codes[:], u_scales[:])
 
         groups = HALF // BUNDLE
         means = []
@@ -182,12 +198,14 @@ def tile_list_steps_levelled_pickgap_pl_kernel(
             nc.vector.tensor_copy(first[:, t, :], p_sb[t][:].indirect(list2[:]))
             nc.scalar.activation(second[:, t, :], p_sb[t][:].indirect(list3[:]), COPY)
         gap = tile("gap", [P, PACK, E], F32)
-        nc.vector.tensor_tensor(gap[:], first[:], second[:], SUB)
-        y = tile("y", [P, PACK, E], F32)
-        nc.vector.tensor_tensor(y[:], gap[:], gm_sb[:].unsqueeze(2).to_broadcast([P, PACK, E]), MULT)
-        nc.sync.dma_start(out_0.rearrange("(p t) e -> p t e", t=PACK), y[:])
         y_bf = tile("y_bf", [P, E, PACK], BF16)
-        nc.vector.tensor_copy(y_bf[:], y[:].rearrange("p t e -> p e t"))
+        y = tile("y", [P, PACK, E], F32)
+        for t0 in (0, 2):
+            nc.vector.tensor_tensor(gap[:, t0 : t0 + 2, :], first[:, t0 : t0 + 2, :], second[:, t0 : t0 + 2, :], SUB)
+        for t in range(PACK):
+            nc.vector.tensor_scalar(y_bf[:, :, t], gap[:, t, :], gm_sb[:, t : t + 1], None, MULT)
+            nc.scalar.activation(y[:, t, :], gap[:, t, :], COPY, scale=gm_sb[:, t : t + 1])
+        nc.sync.dma_start(out_0.rearrange("(p t) e -> p t e", t=PACK), y[:])
         y_codes = tile("y_codes", [P, E], U32)
         y_scales = tile("y_scales", [P, E], U8)
         nc.vector.quantize_mx(y_codes[:].bitcast(E4M3), y_scales[:], y_bf[:].rearrange("p e t -> p (e t)"))

@@ -38,18 +38,16 @@ def tile_list_steps_levelled_pickgap_pl_kernel(
         def tile(name, shape, dtype):
             return sb.tile(shape, dtype, name=name, align_bytes=64)
 
-        list1 = tile("list1", [P, J // 16], U16)
-        nc.sync.dma_start(list1[:], offs)
         scales_raw = tile("scales_raw", [P, R], U8)
         nc.gpsimd.memset(scales_raw[:].bitcast(I32), 0)
         fk_sb = tile("fk_sb", [P, PASSES, PACK], F32)
-        nc.gpsimd.dma_start(fk_sb[:], fk.rearrange("(a p i) o -> p a (i o)", a=PASSES, i=PACK))
+        nc.scalar.dma_start(fk_sb[:], fk.rearrange("(a p i) o -> p a (i o)", a=PASSES, i=PACK))
         gm_sb = tile("gm_sb", [P, PACK], F32)
         nc.gpsimd.dma_start(gm_sb[:], gm.rearrange("(p t) o -> p (t o)", t=PACK))
 
         planes = xf.rearrange("(a p i) t -> a i p t", a=PASSES, i=PACK)
         x_sb = {(a, i): tile("x%d%d" % (a, i), [P, T], F32) for a in range(PASSES) for i in range(PACK)}
-        w_raw = tile("w_raw", [P, PASSES, R], I32)
+        w_raw = [tile("w_raw%d" % a, [P, R], I32) for a in range(PASSES)]
         wb_raw = tile("wb_raw", [P, 2 * N], U8)
 
         def load_plane(a, i):
@@ -66,37 +64,34 @@ def tile_list_steps_levelled_pickgap_pl_kernel(
             )
 
         load_plane(0, 0)
+        list1 = tile("list1", [P, J // 16], U16)
+        nc.sync.dma_start(list1[:], offs)
         load_w_scales(0)
-        nc.sync.dma_start(w_raw[:], w_words.rearrange("a p n t -> p a (n t)").bitcast(I32))
         load_w_scales(1)
-        nc.sync.dma_start(wb_raw[:].bitcast(I32), wb_words[0].bitcast(I32))
-        load_w_scales(2)
         load_plane(0, 1)
+        load_w_scales(2)
         load_w_scales(3)
         load_plane(0, 2)
-        load_wb_scales(0)
-        load_wb_scales(1)
         load_plane(0, 3)
-        load_wb_scales(2)
-        load_wb_scales(3)
+        for q in range(4):
+            load_wb_scales(q)
         for i in range(PACK):
             load_plane(1, i)
+        for a in range(PASSES):
+            nc.sync.dma_start(w_raw[a][:], w_words[a].rearrange("p n t -> p (n t)").bitcast(I32))
+        nc.sync.dma_start(wb_raw[:].bitcast(I32), wb_words[0].bitcast(I32))
         list2 = tile("list2", [P, E // 16], U16)
         nc.sync.dma_start(list2[:], offs2)
         list3 = tile("list3", [P, E // 16], U16)
         nc.sync.dma_start(list3[:], offs3)
 
-        w_dealt = tile("w_dealt", [P, PASSES, R], I32)
-        for a in range(PASSES):
+        w_dealt = [tile("w_dealt%d" % a, [P, R], I32) for a in range(PASSES)]
+
+        def deal(dealt, raw):
             nc.vector.tensor_copy(
-                w_dealt[:, a, :].rearrange("p (t m) -> p m t", t=PACK),
-                w_raw[:, a, :].rearrange("p (m t) -> p m t", t=PACK),
+                dealt.rearrange("p (t m) -> p m t", t=PACK), raw.rearrange("p (m t) -> p m t", t=PACK)
             )
-        wb_dealt = tile("wb_dealt", [P, 2 * N], U8)
-        nc.vector.tensor_copy(
-            wb_dealt[:].bitcast(U16).rearrange("p (t m) -> p m t", t=PACK),
-            wb_raw[:].bitcast(U16).rearrange("p (m t) -> p m t", t=PACK),
-        )
+
         scales_dealt = tile("scales_dealt", [P, R], U8)
         nc.vector.tensor_copy(
             scales_dealt[:].rearrange("p (t m) -> p t m", t=PACK),
@@ -105,7 +100,9 @@ def tile_list_steps_levelled_pickgap_pl_kernel(
 
         acc_a = [ps.tile([P, PACK, HALF], F32, name="acc_a%d" % h) for h in range(2)]
         xg = tile("xg", [P, PASSES * PACK, PAD + J], F32)
-        nc.vector.memset(xg[:, :, PAD - 1 : PAD], 0.0)
+        zeros = tile("zeros", [P, PASSES * PACK, 1], F32)
+        nc.vector.memset(zeros[:], 0.0)
+        nc.scalar.activation(xg[:, :, PAD - 1 : PAD], zeros[:], COPY)
 
         def take_step(dst, row, lo, hi):
             nc.vector.scalar_tensor_tensor(
@@ -117,7 +114,7 @@ def tile_list_steps_levelled_pickgap_pl_kernel(
                 cols = slice(t * P, (t + 1) * P)
                 nc.tensor.matmul_mx(
                     acc_a[h][:, t, :],
-                    lhsT=w_dealt[:, a, cols].bitcast(E4M3),
+                    lhsT=w_dealt[a][:, cols].bitcast(E4M3),
                     lhsT_scale=scales_dealt[4 + 4 * a :, cols],
                     rhs=codes.bitcast(E4M3),
                     rhs_scale=scales,
@@ -126,27 +123,54 @@ def tile_list_steps_levelled_pickgap_pl_kernel(
                 )
 
         steps = tile("steps", [P, PASSES * PACK, J], F32)
+        u_bf, u_codes, u_scales = {}, {}, {}
         for a in range(PASSES):
-            u_bf = [tile("u%d%d" % (a, h), [P, HALF, PACK], BF16) for h in range(2)]
-            for i in range(PACK):
-                row = a * PACK + i
-                window = x_sb[a, i][:]
-                if row == PASSES * PACK - 1:
-                    nc.scalar.activation(xg[:, row, PAD : PAD + HALF], window.indirect(list1[:, 0:8]), COPY)
-                    nc.vector.tensor_copy(xg[:, row, PAD + HALF :], window.indirect(list1[:, 8:16]))
-                else:
-                    nc.scalar.activation(xg[:, row, PAD:], window.indirect(list1[:]), COPY)
-                for h in range(2):
-                    take_step(steps[:, row, h * HALF : (h + 1) * HALF], row, h * HALF, (h + 1) * HALF)
-                for h in range(2):
-                    nc.vector.tensor_scalar(
-                        u_bf[h][:, :, i], steps[:, row, h * HALF : (h + 1) * HALF], fk_sb[:, a, i : i + 1], None, MULT
-                    )
             for h in range(2):
-                u_codes = tile("uc%d%d" % (a, h), [P, HALF], U32)
-                u_scales = tile("us%d%d" % (a, h), [P, HALF], U8)
-                nc.vector.quantize_mx(u_codes[:].bitcast(E4M3), u_scales[:], u_bf[h][:].rearrange("p j t -> p (j t)"))
-                first_product(a, h, u_codes[:], u_scales[:])
+                u_bf[a, h] = tile("u%d%d" % (a, h), [P, HALF, PACK], BF16)
+                u_codes[a, h] = tile("uc%d%d" % (a, h), [P, HALF], U32)
+                u_scales[a, h] = tile("us%d%d" % (a, h), [P, HALF], U8)
+
+        def gather_and_step(a, i):
+            row = a * PACK + i
+            window = x_sb[a, i][:]
+            nc.scalar.activation(xg[:, row, PAD : PAD + HALF], window.indirect(list1[:, 0:8]), COPY)
+            nc.scalar.activation(xg[:, row, PAD + HALF :], window.indirect(list1[:, 8:16]), COPY)
+            for h in range(2):
+                take_step(steps[:, row, h * HALF : (h + 1) * HALF], row, h * HALF, (h + 1) * HALF)
+
+        def scale_and_round(a, i):
+            for h in range(2):
+                nc.vector.tensor_scalar(
+                    u_bf[a, h][:, :, i],
+                    steps[:, a * PACK + i, h * HALF : (h + 1) * HALF],
+                    fk_sb[:, a, i : i + 1],
+                    None,
+                    MULT,
+                )
+
+        def quantise_u(a):
+            for h in range(2):
+                nc.vector.quantize_mx(
+                    u_codes[a, h][:].bitcast(E4M3), u_scales[a, h][:], u_bf[a, h][:].rearrange("p j t -> p (j t)")
+                )
+
+        for i in range(PACK):
+            gather_and_step(0, i)
+            scale_and_round(0, i)
+        quantise_u(0)
+        for i in range(PACK - 1):
+            gather_and_step(1, i)
+            scale_and_round(1, i)
+        gather_and_step(1, PACK - 1)
+        deal(w_dealt[0][:], w_raw[0][:])
+        scale_and_round(1, PACK - 1)
+        deal(w_dealt[1][:], w_raw[1][:])
+        quantise_u(1)
+        for a in range(PASSES):
+            for h in range(2):
+                first_product(a, h, u_codes[a, h][:], u_scales[a, h][:])
+        wb_dealt = tile("wb_dealt", [P, 2 * N], U8)
+        deal(wb_dealt[:].bitcast(U16), wb_raw[:].bitcast(U16))
 
         groups = HALF // BUNDLE
         means = []

@@ -35,15 +35,11 @@ def tile_list_steps_levelled_pickgap_pl_kernel(
         sb = ctx.enter_context(tc.tile_pool(name="sb", bufs=1))
         ps = ctx.enter_context(tc.psum_pool(name="ps", bufs=1))
 
-        def tile(name, shape, dtype):
-            return sb.tile(shape, dtype, name=name, align_bytes=64)
+        def tile(name, shape, dtype, tag=None):
+            return sb.tile(shape, dtype, name=name, tag=tag or name, align_bytes=64)
 
-        scales_raw = tile("scales_raw", [P, R], U8)
-        nc.gpsimd.memset(scales_raw[:].bitcast(I32), 0)
-        fk_sb = tile("fk_sb", [P, PASSES, PACK], F32)
-        nc.scalar.dma_start(fk_sb[:], fk.rearrange("(a p i) o -> p a (i o)", a=PASSES, i=PACK))
-        gm_sb = tile("gm_sb", [P, PACK], F32)
-        nc.gpsimd.dma_start(gm_sb[:], gm.rearrange("(p t) o -> p (t o)", t=PACK))
+        scales_raw = tile("scales_raw", [P, 2, R], U8)
+        nc.gpsimd.memset(scales_raw[:].rearrange("p a n -> p (a n)").bitcast(I32), 0)
 
         planes = xf.rearrange("(a p i) t -> a i p t", a=PASSES, i=PACK)
         x_sb = {(a, i): tile("x%d%d" % (a, i), [P, T], F32) for a in range(PASSES) for i in range(PACK)}
@@ -55,27 +51,28 @@ def tile_list_steps_levelled_pickgap_pl_kernel(
 
         def load_w_scales(q):
             nc.sync.dma_start(
-                scales_raw[32 * q + 4 : 32 * q + 12, :].bitcast(I32), w_scales[:, 4 * q : 4 * q + 4, :].bitcast(I32)
+                scales_raw[32 * q : 32 * q + 8, 0, :].bitcast(I32), w_scales[:, 4 * q : 4 * q + 4, :].bitcast(I32)
             )
 
         def load_wb_scales(q):
             nc.sync.dma_start(
-                scales_raw[32 * q : 32 * q + 4, :].bitcast(I32), wb_scales[0, 4 * q : 4 * q + 4, :].bitcast(I32)
+                scales_raw[32 * q : 32 * q + 4, 1, :].bitcast(I32), wb_scales[0, 4 * q : 4 * q + 4, :].bitcast(I32)
             )
 
         load_plane(0, 0)
         list1 = tile("list1", [P, J // 16], U16)
         nc.sync.dma_start(list1[:], offs)
+        fk_sb = tile("fk_sb", [P, PASSES, PACK], F32)
+        nc.sync.dma_start(fk_sb[:], fk.rearrange("(a p i) o -> p a (i o)", a=PASSES, i=PACK))
         load_w_scales(0)
-        load_w_scales(1)
         load_plane(0, 1)
+        load_w_scales(1)
         load_w_scales(2)
-        load_w_scales(3)
         load_plane(0, 2)
+        load_w_scales(3)
         load_plane(0, 3)
-        for q in range(4):
-            load_wb_scales(q)
         for i in range(PACK):
+            load_wb_scales(i)
             load_plane(1, i)
         for a in range(PASSES):
             nc.sync.dma_start(w_raw[a][:], w_words[a].rearrange("p n t -> p (n t)").bitcast(I32))
@@ -84,6 +81,8 @@ def tile_list_steps_levelled_pickgap_pl_kernel(
         nc.sync.dma_start(list2[:], offs2)
         list3 = tile("list3", [P, E // 16], U16)
         nc.sync.dma_start(list3[:], offs3)
+        gm_sb = tile("gm_sb", [P, PACK], F32)
+        nc.sync.dma_start(gm_sb[:], gm.rearrange("(p t) o -> p (t o)", t=PACK))
 
         w_dealt = [tile("w_dealt%d" % a, [P, R], I32) for a in range(PASSES)]
 
@@ -92,11 +91,8 @@ def tile_list_steps_levelled_pickgap_pl_kernel(
                 dealt.rearrange("p (t m) -> p m t", t=PACK), raw.rearrange("p (m t) -> p m t", t=PACK)
             )
 
-        scales_dealt = tile("scales_dealt", [P, R], U8)
-        nc.vector.tensor_copy(
-            scales_dealt[:].rearrange("p (t m) -> p t m", t=PACK),
-            scales_raw[:].rearrange("p (m t) -> p t m", t=PACK),
-        )
+        w_scales_dealt = tile("w_scales_dealt", [P, R], U8)
+        deal(w_scales_dealt[:], scales_raw[:, 0, :])
 
         acc_a = [ps.tile([P, PACK, HALF], F32, name="acc_a%d" % h) for h in range(2)]
         xg = tile("xg", [P, PASSES * PACK, PAD + J], F32)
@@ -115,19 +111,18 @@ def tile_list_steps_levelled_pickgap_pl_kernel(
                 nc.tensor.matmul_mx(
                     acc_a[h][:, t, :],
                     lhsT=w_dealt[a][:, cols].bitcast(E4M3),
-                    lhsT_scale=scales_dealt[4 + 4 * a :, cols],
+                    lhsT_scale=w_scales_dealt[4 * a :, cols],
                     rhs=codes.bitcast(E4M3),
                     rhs_scale=scales,
                     start=(a == 0 and t == 0),
                     stop=(a == PASSES - 1 and t == PACK - 1),
                 )
 
-        steps = tile("steps", [P, PASSES * PACK, J], F32)
+        steps = {}
         u_bf, u_codes, u_scales = {}, {}, {}
         for a in range(PASSES):
             for h in range(2):
                 u_bf[a, h] = tile("u%d%d" % (a, h), [P, HALF, PACK], BF16)
-                u_codes[a, h] = tile("uc%d%d" % (a, h), [P, HALF], U32)
                 u_scales[a, h] = tile("us%d%d" % (a, h), [P, HALF], U8)
 
         def gather_and_step(a, i):
@@ -135,41 +130,48 @@ def tile_list_steps_levelled_pickgap_pl_kernel(
             window = x_sb[a, i][:]
             nc.scalar.activation(xg[:, row, PAD : PAD + HALF], window.indirect(list1[:, 0:8]), COPY)
             nc.scalar.activation(xg[:, row, PAD + HALF :], window.indirect(list1[:, 8:16]), COPY)
-            for h in range(2):
-                take_step(steps[:, row, h * HALF : (h + 1) * HALF], row, h * HALF, (h + 1) * HALF)
 
-        def scale_and_round(a, i):
-            for h in range(2):
-                nc.vector.tensor_scalar(
-                    u_bf[a, h][:, :, i],
-                    steps[:, a * PACK + i, h * HALF : (h + 1) * HALF],
-                    fk_sb[:, a, i : i + 1],
-                    None,
-                    MULT,
-                )
+        def step_half(a, i, h, tag=None):
+            steps[a, i, h] = tile("step%d%d%d" % (a, i, h), [P, HALF], F32, tag=tag)
+            take_step(steps[a, i, h][:], a * PACK + i, h * HALF, (h + 1) * HALF)
 
-        def quantise_u(a):
+        def scale_and_round(a, i, h):
+            nc.vector.tensor_scalar(u_bf[a, h][:, :, i], steps[a, i, h][:], fk_sb[:, a, i : i + 1], None, MULT)
+
+        def quantise_u(a, h, tag=None):
+            u_codes[a, h] = tile("uc%d%d" % (a, h), [P, HALF], U32, tag=tag)
+            nc.vector.quantize_mx(
+                u_codes[a, h][:].bitcast(E4M3), u_scales[a, h][:], u_bf[a, h][:].rearrange("p j t -> p (j t)")
+            )
+
+        def whole_plane(a, i):
+            gather_and_step(a, i)
             for h in range(2):
-                nc.vector.quantize_mx(
-                    u_codes[a, h][:].bitcast(E4M3), u_scales[a, h][:], u_bf[a, h][:].rearrange("p j t -> p (j t)")
-                )
+                step_half(a, i, h)
+            for h in range(2):
+                scale_and_round(a, i, h)
 
         for i in range(PACK):
-            gather_and_step(0, i)
-            scale_and_round(0, i)
-        quantise_u(0)
+            whole_plane(0, i)
+        for h in range(2):
+            quantise_u(0, h)
         for i in range(PACK - 1):
-            gather_and_step(1, i)
-            scale_and_round(1, i)
+            whole_plane(1, i)
         gather_and_step(1, PACK - 1)
+        step_half(1, PACK - 1, 0)
         deal(w_dealt[0][:], w_raw[0][:])
-        scale_and_round(1, PACK - 1)
+        scale_and_round(1, PACK - 1, 0)
+        step_half(1, PACK - 1, 1, tag="w_raw0")
         deal(w_dealt[1][:], w_raw[1][:])
-        quantise_u(1)
+        quantise_u(1, 0, tag="w_raw1")
+        scale_and_round(1, PACK - 1, 1)
+        quantise_u(1, 1)
         for a in range(PASSES):
             for h in range(2):
                 first_product(a, h, u_codes[a, h][:], u_scales[a, h][:])
-        wb_dealt = tile("wb_dealt", [P, 2 * N], U8)
+        wb_scales_dealt = tile("wb_scales_dealt", [P, N], U8, tag="u10")
+        deal(wb_scales_dealt[:], scales_raw[:, 1, :])
+        wb_dealt = tile("wb_dealt", [P, 2 * N], U8, tag="u11")
         deal(wb_dealt[:].bitcast(U16), wb_raw[:].bitcast(U16))
 
         groups = HALF // BUNDLE
@@ -202,7 +204,7 @@ def tile_list_steps_levelled_pickgap_pl_kernel(
                 nc.tensor.matmul_mx(
                     target,
                     lhsT=wb_dealt[:, 2 * t * P : 2 * (t + 1) * P].bitcast(E2M1),
-                    lhsT_scale=scales_dealt[:, t * P : (t + 1) * P],
+                    lhsT_scale=wb_scales_dealt[:, t * P : (t + 1) * P],
                     rhs=h_codes[:].bitcast(E5M2),
                     rhs_scale=h_scales[:],
                     start=True,

@@ -23,8 +23,10 @@ P = 128
 PACK = 4
 PASSES = K // (P * PACK)
 HALF = J // 2
+HALF_COLS = HALF // 16
 BUNDLE = 8
 PAD = 8
+QUADS = 4
 
 
 def tile_list_steps_levelled_pickgap_pl_kernel(
@@ -72,10 +74,11 @@ def tile_list_steps_levelled_pickgap_pl_kernel(
         load_w_scales(3)
         load_plane(0, 3)
         for i in range(PACK):
-            load_wb_scales(i)
             load_plane(1, i)
         for a in range(PASSES):
             nc.sync.dma_start(w_raw[a][:], w_words[a].rearrange("p n t -> p (n t)").bitcast(I32))
+        for q in range(QUADS):
+            load_wb_scales(q)
         nc.sync.dma_start(wb_raw[:].bitcast(I32), wb_words[0].bitcast(I32))
         list2 = tile("list2", [P, E // 16], U16)
         nc.sync.dma_start(list2[:], offs2)
@@ -100,20 +103,15 @@ def tile_list_steps_levelled_pickgap_pl_kernel(
         nc.vector.memset(zeros[:], 0.0)
         nc.scalar.activation(xg[:, :, PAD - 1 : PAD], zeros[:], COPY)
 
-        def take_step(dst, row, lo, hi):
-            nc.vector.scalar_tensor_tensor(
-                dst, xg[:, row, PAD - 1 + lo : PAD - 1 + hi], -0.6, xg[:, row, PAD + lo : PAD + hi], MULT, ADD
-            )
-
-        def first_product(a, h, codes, scales):
+        def first_product(a, h):
             for t in range(PACK):
                 cols = slice(t * P, (t + 1) * P)
                 nc.tensor.matmul_mx(
                     acc_a[h][:, t, :],
                     lhsT=w_dealt[a][:, cols].bitcast(E4M3),
                     lhsT_scale=w_scales_dealt[4 * a :, cols],
-                    rhs=codes.bitcast(E4M3),
-                    rhs_scale=scales,
+                    rhs=u_codes[a, h][:].bitcast(E4M3),
+                    rhs_scale=u_scales[a, h][:],
                     start=(a == 0 and t == 0),
                     stop=(a == PASSES - 1 and t == PACK - 1),
                 )
@@ -125,15 +123,20 @@ def tile_list_steps_levelled_pickgap_pl_kernel(
                 u_bf[a, h] = tile("u%d%d" % (a, h), [P, HALF, PACK], BF16)
                 u_scales[a, h] = tile("us%d%d" % (a, h), [P, HALF], U8)
 
-        def gather_and_step(a, i):
-            row = a * PACK + i
-            window = x_sb[a, i][:]
-            nc.scalar.activation(xg[:, row, PAD : PAD + HALF], window.indirect(list1[:, 0:8]), COPY)
-            nc.scalar.activation(xg[:, row, PAD + HALF :], window.indirect(list1[:, 8:16]), COPY)
+        def gather_plane(a, i):
+            for h in range(2):
+                nc.scalar.activation(
+                    xg[:, a * PACK + i, PAD + h * HALF : PAD + (h + 1) * HALF],
+                    x_sb[a, i][:].indirect(list1[:, h * HALF_COLS : (h + 1) * HALF_COLS]),
+                    COPY,
+                )
 
         def step_half(a, i, h, tag=None):
             steps[a, i, h] = tile("step%d%d%d" % (a, i, h), [P, HALF], F32, tag=tag)
-            take_step(steps[a, i, h][:], a * PACK + i, h * HALF, (h + 1) * HALF)
+            row, lo = a * PACK + i, PAD + h * HALF
+            nc.vector.scalar_tensor_tensor(
+                steps[a, i, h][:], xg[:, row, lo - 1 : lo - 1 + HALF], -0.6, xg[:, row, lo : lo + HALF], MULT, ADD
+            )
 
         def scale_and_round(a, i, h):
             nc.vector.tensor_scalar(u_bf[a, h][:, :, i], steps[a, i, h][:], fk_sb[:, a, i : i + 1], None, MULT)
@@ -145,7 +148,7 @@ def tile_list_steps_levelled_pickgap_pl_kernel(
             )
 
         def whole_plane(a, i):
-            gather_and_step(a, i)
+            gather_plane(a, i)
             for h in range(2):
                 step_half(a, i, h)
             for h in range(2):
@@ -157,18 +160,19 @@ def tile_list_steps_levelled_pickgap_pl_kernel(
             quantise_u(0, h)
         for i in range(PACK - 1):
             whole_plane(1, i)
-        gather_and_step(1, PACK - 1)
-        step_half(1, PACK - 1, 0)
+        last = PACK - 1
+        gather_plane(1, last)
+        step_half(1, last, 0)
         deal(w_dealt[0][:], w_raw[0][:])
-        scale_and_round(1, PACK - 1, 0)
-        step_half(1, PACK - 1, 1, tag="w_raw0")
+        scale_and_round(1, last, 0)
+        step_half(1, last, 1, tag="w_raw0")
         deal(w_dealt[1][:], w_raw[1][:])
         quantise_u(1, 0, tag="w_raw1")
-        scale_and_round(1, PACK - 1, 1)
+        scale_and_round(1, last, 1)
         quantise_u(1, 1)
         for a in range(PASSES):
             for h in range(2):
-                first_product(a, h, u_codes[a, h][:], u_scales[a, h][:])
+                first_product(a, h)
         wb_scales_dealt = tile("wb_scales_dealt", [P, N], U8, tag="u10")
         deal(wb_scales_dealt[:], scales_raw[:, 1, :])
         wb_dealt = tile("wb_dealt", [P, 2 * N], U8, tag="u11")
@@ -176,13 +180,13 @@ def tile_list_steps_levelled_pickgap_pl_kernel(
 
         groups = HALF // BUNDLE
         means = []
+        sums = tile("sums", [P, 2, groups, PACK], F32, tag="wb_raw")
         for h in range(2):
-            sums = tile("sums%d" % h, [P, groups, PACK], F32)
             nc.vector.tensor_reduce(
-                sums[:], acc_a[h][:].rearrange("p t (g s) -> p g t s", s=BUNDLE), mybir.AxisListType.X, ADD
+                sums[:, h], acc_a[h][:].rearrange("p t (g s) -> p g t s", s=BUNDLE), mybir.AxisListType.X, ADD
             )
             mean = tile("mean%d" % h, [P, groups, PACK], F32)
-            nc.scalar.activation(mean[:], sums[:], COPY, scale=1.0 / BUNDLE)
+            nc.scalar.activation(mean[:], sums[:, h], COPY, scale=1.0 / BUNDLE)
             means.append(mean)
 
         p_sb = [tile("p%d" % t, [P, J], F32) for t in range(PACK)]
@@ -226,7 +230,7 @@ def tile_list_steps_levelled_pickgap_pl_kernel(
         gap = tile("gap", [P, PACK, E], F32)
         y_bf = tile("y_bf", [P, E, PACK], BF16)
         y = tile("y", [P, PACK, E], F32)
-        for t0 in (0, 2):
+        for t0 in range(0, PACK, 2):
             nc.vector.tensor_tensor(gap[:, t0 : t0 + 2, :], first[:, t0 : t0 + 2, :], second[:, t0 : t0 + 2, :], SUB)
         for t in range(PACK):
             nc.vector.tensor_scalar(y_bf[:, :, t], gap[:, t, :], gm_sb[:, t : t + 1], None, MULT)
@@ -236,7 +240,7 @@ def tile_list_steps_levelled_pickgap_pl_kernel(
         y_scales = tile("y_scales", [P, E], U8)
         nc.vector.quantize_mx(y_codes[:].bitcast(E4M3), y_scales[:], y_bf[:].rearrange("p e t -> p (e t)"))
         nc.scalar.dma_start(out_1[0].rearrange("p c r -> p (c r)").bitcast(I32), y_codes[:].bitcast(I32))
-        for q in range(4):
+        for q in range(QUADS):
             queue = nc.sync if q % 2 == 0 else nc.scalar
             queue.dma_start(
                 out_2[0, 4 * q : 4 * q + 4, :].bitcast(I32), y_scales[32 * q : 32 * q + 4, :].bitcast(I32)

from contextlib import ExitStack

import concourse.mybir as mybir

K, T, J, R, N, E = 1024, 1024, 256, 512, 512, 64
FLOPS = 2 * K * R * J + 2 * R * N * J

F32 = mybir.dt.float32
BF16 = mybir.dt.bfloat16
I32 = mybir.dt.int32
U32 = mybir.dt.uint32
U16 = mybir.dt.uint16
U8 = mybir.dt.uint8
E4M3 = mybir.dt.float8_e4m3fn_x4
E5M2 = mybir.dt.float8_e5m2_x4
E2M1 = mybir.dt.float4_e2m1fn_x4
MULT = mybir.AluOpType.mult
ADD = mybir.AluOpType.add
SUB = mybir.AluOpType.subtract
COPY = mybir.ActivationFunctionType.Copy

P = 128
PACK = 4
PASSES = K // (P * PACK)
HALF = J // 2
HALF_COLS = HALF // 16
BUNDLE = 8
PAD = 8
QUADS = 4


def tile_list_steps_levelled_pickgap_pl_kernel(
    tc, xf, fk, w_words, w_scales, wb_words, wb_scales, gm, offs, offs2, offs3, out_0, out_1, out_2
):
    nc = tc.nc
    with ExitStack() as ctx:
        sb = ctx.enter_context(tc.tile_pool(name="sb", bufs=1))
        ps = ctx.enter_context(tc.psum_pool(name="ps", bufs=1))

        def tile(name, shape, dtype, tag=None):
            return sb.tile(shape, dtype, name=name, tag=tag or name, align_bytes=64)

        scales_raw = tile("scales_raw", [P, 2, R], U8)
        nc.gpsimd.memset(scales_raw[:].rearrange("p a n -> p (a n)").bitcast(I32), 0)

        planes = xf.rearrange("(a p i) t -> a i p t", a=PASSES, i=PACK)
        x_sb = {(a, i): tile("x%d%d" % (a, i), [P, T], F32) for a in range(PASSES) for i in range(PACK)}
        w_raw = [tile("w_raw%d" % a, [P, R], I32) for a in range(PASSES)]
        wb_raw = tile("wb_raw", [P, 2 * N], U8)

        def load_plane(a, i):
            nc.sync.dma_start(x_sb[a, i][:], planes[a, i])

        def load_w_scales(q):
            nc.sync.dma_start(
                scales_raw[32 * q : 32 * q + 8, 0, :].bitcast(I32), w_scales[:, 4 * q : 4 * q + 4, :].bitcast(I32)
            )

        def load_wb_scales(q):
            nc.sync.dma_start(
                scales_raw[32 * q : 32 * q + 4, 1, :].bitcast(I32), wb_scales[0, 4 * q : 4 * q + 4, :].bitcast(I32)
            )

        load_plane(0, 0)
        list1 = tile("list1", [P, J // 16], U16)
        nc.sync.dma_start(list1[:], offs)
        fk_sb = tile("fk_sb", [P, PASSES, PACK], F32)
        nc.sync.dma_start(fk_sb[:], fk.rearrange("(a p i) o -> p a (i o)", a=PASSES, i=PACK))
        load_w_scales(0)
        load_plane(0, 1)
        load_w_scales(1)
        load_w_scales(2)
        load_plane(0, 2)
        load_w_scales(3)
        load_plane(0, 3)
        for i in range(PACK):
            load_plane(1, i)
        for a in range(PASSES):
            nc.sync.dma_start(w_raw[a][:], w_words[a].rearrange("p n t -> p (n t)").bitcast(I32))
        for q in range(QUADS):
            load_wb_scales(q)
        nc.sync.dma_start(wb_raw[:].bitcast(I32), wb_words[0].bitcast(I32))
        list2 = tile("list2", [P, E // 16], U16)
        nc.sync.dma_start(list2[:], offs2)
        list3 = tile("list3", [P, E // 16], U16)
        nc.sync.dma_start(list3[:], offs3)
        gm_sb = tile("gm_sb", [P, PACK], F32)
        nc.sync.dma_start(gm_sb[:], gm.rearrange("(p t) o -> p (t o)", t=PACK))

        w_dealt = [tile("w_dealt%d" % a, [P, R], I32) for a in range(PASSES)]

        def deal(dealt, raw):
            nc.vector.tensor_copy(
                dealt.rearrange("p (t m) -> p m t", t=PACK), raw.rearrange("p (m t) -> p m t", t=PACK)
            )

        w_scales_dealt = tile("w_scales_dealt", [P, R], U8)
        deal(w_scales_dealt[:], scales_raw[:, 0, :])

        acc_a = [ps.tile([P, PACK, HALF], F32, name="acc_a%d" % h) for h in range(2)]
        xg = tile("xg", [P, PASSES * PACK, PAD + J], F32)
        zeros = tile("zeros", [P, PASSES * PACK, 1], F32)
        nc.vector.memset(zeros[:], 0.0)
        nc.scalar.activation(xg[:, :, PAD - 1 : PAD], zeros[:], COPY)

        def first_product(a, h):
            for t in range(PACK):
                cols = slice(t * P, (t + 1) * P)
                nc.tensor.matmul_mx(
                    acc_a[h][:, t, :],
                    lhsT=w_dealt[a][:, cols].bitcast(E4M3),
                    lhsT_scale=w_scales_dealt[4 * a :, cols],
                    rhs=u_codes[a, h][:].bitcast(E4M3),
                    rhs_scale=u_scales[a, h][:],
                    start=(a == 0 and t == 0),
                    stop=(a == PASSES - 1 and t == PACK - 1),
                )

        steps = {}
        u_bf, u_codes, u_scales = {}, {}, {}
        for a in range(PASSES):
            for h in range(2):
                u_bf[a, h] = tile("u%d%d" % (a, h), [P, HALF, PACK], BF16)
                u_scales[a, h] = tile("us%d%d" % (a, h), [P, HALF], U8)

        def gather_plane(a, i):
            for h in range(2):
                nc.scalar.activation(
                    xg[:, a * PACK + i, PAD + h * HALF : PAD + (h + 1) * HALF],
                    x_sb[a, i][:].indirect(list1[:, h * HALF_COLS : (h + 1) * HALF_COLS]),
                    COPY,
                )

        def step_half(a, i, h, tag=None):
            steps[a, i, h] = tile("step%d%d%d" % (a, i, h), [P, HALF], F32, tag=tag)
            row, lo = a * PACK + i, PAD + h * HALF
            nc.vector.scalar_tensor_tensor(
                steps[a, i, h][:], xg[:, row, lo - 1 : lo - 1 + HALF], -0.6, xg[:, row, lo : lo + HALF], MULT, ADD
            )

        def scale_and_round(a, i, h):
            nc.vector.tensor_scalar(u_bf[a, h][:, :, i], steps[a, i, h][:], fk_sb[:, a, i : i + 1], None, MULT)

        def quantise_u(a, h, tag=None):
            u_codes[a, h] = tile("uc%d%d" % (a, h), [P, HALF], U32, tag=tag)
            nc.vector.quantize_mx(
                u_codes[a, h][:].bitcast(E4M3), u_scales[a, h][:], u_bf[a, h][:].rearrange("p j t -> p (j t)")
            )

        def whole_plane(a, i):
            gather_plane(a, i)
            for h in range(2):
                step_half(a, i, h)
            for h in range(2):
                scale_and_round(a, i, h)

        for i in range(PACK):
            whole_plane(0, i)
        for h in range(2):
            quantise_u(0, h)
        for i in range(PACK - 1):
            whole_plane(1, i)
        last = PACK - 1
        gather_plane(1, last)
        step_half(1, last, 0)
        deal(w_dealt[0][:], w_raw[0][:])
        scale_and_round(1, last, 0)
        step_half(1, last, 1, tag="w_raw0")
        deal(w_dealt[1][:], w_raw[1][:])
        quantise_u(1, 0, tag="w_raw1")
        scale_and_round(1, last, 1)
        quantise_u(1, 1)
        for a in range(PASSES):
            for h in range(2):
                first_product(a, h)
        wb_scales_dealt = tile("wb_scales_dealt", [P, N], U8, tag="u10")
        deal(wb_scales_dealt[:], scales_raw[:, 1, :])
        wb_dealt = tile("wb_dealt", [P, 2 * N], U8, tag="u11")
        deal(wb_dealt[:].bitcast(U16), wb_raw[:].bitcast(U16))

        groups = HALF // BUNDLE
        means = []
        sums = tile("sums", [P, 2, groups, PACK], F32, tag="wb_raw")
        for h in range(2):
            nc.vector.tensor_reduce(
                sums[:, h], acc_a[h][:].rearrange("p t (g s) -> p g t s", s=BUNDLE), mybir.AxisListType.X, ADD
            )
            mean = tile("mean%d" % h, [P, groups, PACK], F32)
            nc.scalar.activation(mean[:], sums[:, h], COPY, scale=1.0 / BUNDLE)
            means.append(mean)

        p_sb = [tile("p%d" % t, [P, J], F32) for t in range(PACK)]
        acc_p0 = ps.tile([P, PACK, HALF], F32, name="acc_p0")
        acc_p1 = [ps.tile([P, HALF], F32, name="acc_p1%d" % t) for t in range(PACK)]
        for h in range(2):
            hid_bf = tile("hid%d" % h, [P, HALF, PACK], BF16)
            nc.vector.tensor_tensor(
                hid_bf[:].rearrange("p (g s) t -> p g s t", s=BUNDLE),
                acc_a[h][:].rearrange("p t (g s) -> p g s t", s=BUNDLE),
                means[h][:].unsqueeze(2).to_broadcast([P, groups, BUNDLE, PACK]),
                SUB,
            )
            h_codes = tile("hc%d" % h, [P, HALF], U32)
            h_scales = tile("hs%d" % h, [P, HALF], U8)
            nc.vector.quantize_mx(h_codes[:].bitcast(E5M2), h_scales[:], hid_bf[:].rearrange("p j t -> p (j t)"))
            for t in range(PACK):
                target = acc_p0[:, t, :] if h == 0 else acc_p1[t][:]
                nc.tensor.matmul_mx(
                    target,
                    lhsT=wb_dealt[:, 2 * t * P : 2 * (t + 1) * P].bitcast(E2M1),
                    lhsT_scale=wb_scales_dealt[:, t * P : (t + 1) * P],
                    rhs=h_codes[:].bitcast(E5M2),
                    rhs_scale=h_scales[:],
                    start=True,
                    stop=True,
                )
            for t in range(PACK):
                if h == 0:
                    nc.scalar.copy(p_sb[t][:, :HALF], acc_p0[:, t, :])
                elif t % 2 == 0:
                    nc.vector.tensor_copy(p_sb[t][:, HALF:], acc_p1[t][:])
                else:
                    nc.scalar.copy(p_sb[t][:, HALF:], acc_p1[t][:])

        first = tile("first", [P, PACK, E], F32)
        second = tile("second", [P, PACK, E], F32)
        for t in range(PACK):
            nc.vector.tensor_copy(first[:, t, :], p_sb[t][:].indirect(list2[:]))
            nc.scalar.activation(second[:, t, :], p_sb[t][:].indirect(list3[:]), COPY)
        gap = tile("gap", [P, PACK, E], F32)
        y_bf = tile("y_bf", [P, E, PACK], BF16)
        y = tile("y", [P, PACK, E], F32)
        for t0 in range(0, PACK, 2):
            nc.vector.tensor_tensor(gap[:, t0 : t0 + 2, :], first[:, t0 : t0 + 2, :], second[:, t0 : t0 + 2, :], SUB)
        for t in range(PACK):
            nc.vector.tensor_scalar(y_bf[:, :, t], gap[:, t, :], gm_sb[:, t : t + 1], None, MULT)
            nc.scalar.activation(y[:, t, :], gap[:, t, :], COPY, scale=gm_sb[:, t : t + 1])
        nc.sync.dma_start(out_0.rearrange("(p t) e -> p t e", t=PACK), y[:])
        y_codes = tile("y_codes", [P, E], U32)
        y_scales = tile("y_scales", [P, E], U8)
        nc.vector.quantize_mx(y_codes[:].bitcast(E4M3), y_scales[:], y_bf[:].rearrange("p e t -> p (e t)"))
        nc.scalar.dma_start(out_1[0].rearrange("p c r -> p (c r)").bitcast(I32), y_codes[:].bitcast(I32))
        for q in range(QUADS):
            queue = nc.sync if q % 2 == 0 else nc.scalar
            queue.dma_start(
                out_2[0, 4 * q : 4 * q + 4, :].bitcast(I32), y_scales[32 * q : 32 * q + 4, :].bitcast(I32)
            )
